import numpy as np
import ml_dtypes


def mxq(x, axis, fmt="e4m3"):
    dtype, down = {"e4m3": (ml_dtypes.float8_e4m3fn, 7), "e5m2": (ml_dtypes.float8_e5m2, 14)}[fmt]
    v = np.moveaxis(np.asarray(x, np.float32).astype(ml_dtypes.bfloat16).astype(np.float64), axis, -1)
    blocks = v.reshape(v.shape[:-1] + (-1, 32))
    amax = np.abs(blocks).max(-1, keepdims=True)
    byte = np.maximum(np.where(amax > 0, np.frexp(amax)[1] - 1 + 127, 0) - down, 1)
    scale = np.exp2(byte - 127.0)
    codes = (blocks / scale).astype(np.float32).astype(dtype).astype(np.float64)
    return np.moveaxis((codes * scale).reshape(v.shape), -1, axis)


WIDE = False


def mx_kscale(k, group=512):
    if not WIDE:
        return np.ones(k)
    levels = np.array([10, -10, 5, -5, 0])
    if group != 512:
        return np.exp2(np.random.permutation(np.resize(levels, k // group))).repeat(group)
    if k % 512:
        return np.exp2(np.random.permutation(np.resize(levels, k // 32))).repeat(32)
    a = np.empty((k // 512, 16))
    for p in range(k // 512):
        a[p, :8] = np.random.permutation(np.resize(levels, 8))
        for g in range(8):
            far = levels[np.abs(levels - a[p, g]) >= 10]
            a[p, g + 8] = far[np.random.randint(len(far))]
    return np.exp2(a.ravel()).repeat(32)


def f64(x):
    return np.asarray(x).astype(np.float64)


def striped(idx):
    return np.tile(np.asarray(idx).reshape(-1, 16).T, (8, 1)).astype(np.uint16)


def unstriped(offs):
    return offs[:16].T.reshape(-1).astype(np.int64)


H, KV, D, NQ, N = 4, 1, 256, 512, 512


def setup_inputs():
    n = np.random.standard_normal
    s = mx_kscale(D, 0)[:, None]
    u = mx_kscale(N)
    t = np.random.uniform(0.5, 2.0, N) * u
    v = n((KV, N, 128))
    return {
        "qT": (n((H, D, NQ)) * s * (0.70 / np.sqrt(D))).astype(np.float32),
        "kT": (n((KV, D, N)) / s).astype(np.float32),
        "t": t.reshape(N, 1).astype(np.float32),
        "v": (v / t[:, None]).astype(np.float32),
        "kb": (0.5 * n((N, 1))).astype(np.float32),
        "mask": (np.arange(N)[:, None] <= np.sort(np.random.randint(N // 4, N, NQ))[None, :]).astype(np.float32),
        "gn": np.tile(np.random.uniform(0.5, 2.0, 128), (128, 1)).astype(np.float32),
    }


def reference(qT, kT, t, v, kb, mask, gn):
    a = np.repeat(mxq(f64(kT), 1, "e4m3"), H // KV, 0).transpose(0, 2, 1) @ mxq(f64(qT), 1, "e4m3")
    a = a + f64(kb)
    p = 1.0 / (1.0 + np.exp(-a))
    p = p * f64(mask)
    w = p * f64(t)
    y = mxq(w, 1, "e4m3").transpose(0, 2, 1) @ np.repeat(mxq(f64(v), 1, "e4m3"), H // KV, 0)
    y = y / 16.0
    y = y / np.sqrt(np.mean(np.square(y), -1, keepdims=True) + 1e-5) * f64(gn)[:1]
    return y

@@ -1,0 +1,310 @@
+from contextlib import ExitStack
+
+import concourse.mybir as mybir
+
+H, D, NQ, N, E = 4, 256, 512, 512, 128
+FLOPS = 2 * H * N * NQ * D + 2 * H * NQ * N * E
+
+F32 = mybir.dt.float32
+BF16 = mybir.dt.bfloat16
+U32 = mybir.dt.uint32
+U8 = mybir.dt.uint8
+FP8X4 = mybir.dt.float8_e4m3fn_x4
+ACT = mybir.ActivationFunctionType
+ALU = mybir.AluOpType
+
+P = 128
+ROWS = 64
+PACK = 4
+Q = 128
+EPS = 1e-5
+
+
+def tile_rows_a_sigmoid_kb_mask_onorm_kernel(tc, qT, kT, t, v, kb, mask, gn, out):
+    nc = tc.nc
+    with ExitStack() as ctx:
+        sb = ctx.enter_context(tc.tile_pool(name="sb", bufs=1))
+        ps = ctx.enter_context(tc.psum_pool(name="ps", bufs=1))
+        ctx.enter_context(tc.manual_schedule())
+
+        def sbuf(name, shape, dtype):
+            return sb.tile(shape, dtype, name=name, align_bytes=64)
+
+        spans = [(0, 1), (1, 1), (2, 2)]
+        span_of = {0: 0, 1: 1, 2: 2, 3: 2}
+
+        k_raw = [sbuf("k_raw%d" % i, [P, PACK, N // 2], F32) for i in range(2)]
+        k_bf = [sbuf("k_bf%d" % i, [P, 2, P, PACK], BF16) for i in range(2)]
+        k_codes = [sbuf("k_codes%d" % i, [P, 2 * P], U32) for i in range(2)]
+        k_scales = [sbuf("k_scales%d" % i, [P, 2 * P], U8) for i in range(2)]
+        q_raw, q_bf, q_codes, q_scales = {}, {}, {}, {}
+        for pair in range(2):
+            for s, (c0, nch) in enumerate(spans):
+                w = nch * Q
+                q_raw[pair, s] = sbuf("q_raw%d%d" % (pair, s), [P, PACK, w], F32)
+                q_bf[pair, s] = sbuf("q_bf%d%d" % (pair, s), [P, w, PACK], BF16)
+                q_codes[pair, s] = sbuf("q_codes%d%d" % (pair, s), [P, w], U32)
+                q_scales[pair, s] = sbuf("q_scales%d%d" % (pair, s), [P, w], U8)
+        m_raw = [sbuf("m_raw%d" % s, [P, PACK, nch * Q], F32) for s, (c0, nch) in enumerate(spans)]
+        tm = [sbuf("tm%d" % s, [P, PACK, nch * Q], F32) for s, (c0, nch) in enumerate(spans)]
+        v_raw = sbuf("v_raw", [P, PACK, E], F32)
+        v_bf = sbuf("v_bf", [P, E, PACK], BF16)
+        v_codes = sbuf("v_codes", [P, E], U32)
+        v_scales = sbuf("v_scales", [P, E], U8)
+        kb_sb = sbuf("kb_sb", [P, PACK], F32)
+        t_sb = sbuf("t_sb", [P, PACK], F32)
+        gn_sb = sbuf("gn_sb", [P, E], F32)
+        warm_in = sbuf("warm_in", [P, 1], F32)
+        warm_out = sbuf("warm_out", [P, 1], F32)
+
+        units = [[(0, 0)], [(1, 0)], [(0, 1), (1, 1)], [(0, 2), (0, 3)], [(1, 2), (1, 3)]]
+        groups = []
+        for u, members in enumerate(units):
+            for g in range(2):
+                for m, (pair, c) in enumerate(members):
+                    groups.append((u, g, m, 2 * pair + g, c))
+        p_sb = {}
+        for u, members in enumerate(units):
+            for g in range(2):
+                p_sb[u, g] = sbuf("p%d%d" % (u, g), [P, PACK, len(members) * Q], F32)
+        w_bf = [sbuf("w_bf%d" % k, [P, Q, PACK], BF16) for k in range(16)]
+        w_codes = [sbuf("w_codes%d" % k, [P, Q], U32) for k in range(16)]
+        w_scales = [sbuf("w_scales%d" % k, [P, Q], U8) for k in range(16)]
+        squares = sbuf("squares", [P, 16, E], BF16)
+        batches = [[0, 1, 2, 3], [4, 5, 6, 7], [8, 9], [10, 11], [12, 13], [14, 15]]
+        y_place = {}
+        for b, (bank, slot) in enumerate([(0, 0), (1, 0), (2, 0), (3, 0), (2, 2), (3, 2)]):
+            for i, k in enumerate(batches[b]):
+                y_place[k] = (bank, slot + i)
+        ssq = [sbuf("ssq%d" % b, [P, len(ks)], F32) for b, ks in enumerate(batches)]
+        rstd = [sbuf("rstd%d" % b, [P, len(ks)], F32) for b, ks in enumerate(batches)]
+        o_sb = [sbuf("o%d" % b, [P, len(ks), E], F32) for b, ks in enumerate(batches)]
+
+        s_ps = {}
+        for g in range(2):
+            for i in range(2):
+                s_ps[g, i] = ps.tile([P, 4 * Q], F32, name="s%d%d" % (g, i))
+        y_ps = [ps.tile([P, 4, E], F32, name="y%d" % i) for i in range(4)]
+
+        k_view = kT[0].rearrange("(p j) n -> p j n", j=PACK)
+
+        def load_k(half):
+            cols = slice(half * N // 2, (half + 1) * N // 2)
+            nc.sync.dma_start(out=k_raw[half][0:ROWS], in_=k_view[:, :, cols])
+            nc.scalar.dma_start(out=k_raw[half][ROWS:P], in_=k_view[:, :, cols])
+
+        def load_q(pair, s):
+            c0, nch = spans[s]
+            src = qT[2 * pair : 2 * pair + 2].rearrange("h (p j) n -> (h p) j n", j=PACK)
+            nc.sync.dma_start(out=q_raw[pair, s][:], in_=src[:, :, c0 * Q : (c0 + nch) * Q])
+
+        def load_mask(s):
+            c0, nch = spans[s]
+            src = mask.rearrange("(p r) n -> p r n", r=PACK)
+            nc.sync.dma_start(out=m_raw[s][:], in_=src[:, :, c0 * Q : (c0 + nch) * Q])
+
+        def cast(eng, dst, src):
+            if eng == "v":
+                nc.vector.tensor_copy(out=dst, in_=src)
+            else:
+                nc.scalar.copy(out=dst, in_=src)
+
+        def cast_k(eng, half, i):
+            src = k_raw[half][:].rearrange("p j (s r) -> p s j r", r=PACK)[:, :, :, 2 * i : 2 * i + 2]
+            dst = k_bf[i][:, :, half * ROWS : (half + 1) * ROWS, :].rearrange("p r s j -> p s j r")
+            cast(eng, dst, src)
+
+        def interleave(eng, dst, src):
+            cast(eng, dst.rearrange("p (c i) j -> p c j i", i=2), src.rearrange("p j (c i) -> p c j i", i=2))
+
+        def quant(codes, scales, src):
+            nc.vector.quantize_mx(out=codes.bitcast(FP8X4), scales=scales, in_=src)
+
+        def quant_k(i):
+            quant(k_codes[i][:], k_scales[i][:], k_bf[i][:].rearrange("p r s j -> p (r s j)"))
+
+        def cast_q(eng, pair, s):
+            interleave(eng, q_bf[pair, s][:], q_raw[pair, s][:])
+
+        def quant_q(pair, s):
+            quant(q_codes[pair, s][:], q_scales[pair, s][:], q_bf[pair, s][:].rearrange("p c j -> p (c j)"))
+
+        def make_tm(eng, s):
+            for r in range(PACK):
+                if eng == "v":
+                    nc.vector.tensor_scalar(out=tm[s][:, r, :], in0=m_raw[s][:, r, :], scalar1=t_sb[:, r : r + 1], scalar2=None, op0=ALU.mult)
+                else:
+                    nc.scalar.activation(out=tm[s][:, r, :], in_=m_raw[s][:, r, :], func=ACT.Copy, scale=t_sb[:, r : r + 1])
+
+        def fills(u):
+            if len(units[u]) == 1:
+                return [(u % 2, [0, 1, 2, 3])]
+            return [(0, [0, 1]), (1, [2, 3])]
+
+        def scores(u, f):
+            bank, rs = fills(u)[f]
+            width = len(units[u]) * Q
+            for i, r in enumerate(rs):
+                for m, (pair, c) in enumerate(units[u]):
+                    s = span_of[c]
+                    qcols = slice((c - spans[s][0]) * Q, (c - spans[s][0] + 1) * Q)
+                    kcols = slice((r % 2) * P, (r % 2 + 1) * P)
+                    for g in range(2):
+                        rows = slice(g * ROWS, (g + 1) * ROWS)
+                        nc.tensor.matmul_mx(
+                            out=s_ps[g, bank][:, i * width + m * Q : i * width + (m + 1) * Q],
+                            lhsT=k_codes[r // 2][rows, kcols].bitcast(FP8X4),
+                            lhsT_scale=k_scales[r // 2][rows, kcols],
+                            rhs=q_codes[pair, s][rows, qcols].bitcast(FP8X4),
+                            rhs_scale=q_scales[pair, s][rows, qcols],
+                            start=True,
+                            stop=True,
+                        )
+
+        def sigmoids(u, f):
+            bank, rs = fills(u)[f]
+            width = len(units[u]) * Q
+            for g in range(2):
+                for i, r in enumerate(rs):
+                    nc.scalar.activation(
+                        out=p_sb[u, g][:, r, :],
+                        in_=s_ps[g, bank][:, i * width : (i + 1) * width],
+                        func=ACT.Sigmoid,
+                        bias=kb_sb[:, r : r + 1],
+                    )
+
+        def weigh(k):
+            u, g, m, h, c = groups[k]
+            s = span_of[c]
+            c_in = c - spans[s][0]
+            nc.vector.tensor_tensor(
+                out=w_bf[k][:].rearrange("p (c i) r -> p c r i", i=2),
+                in0=p_sb[u, g][:, :, m * Q : (m + 1) * Q].rearrange("p r (c i) -> p c r i", i=2),
+                in1=tm[s][:, :, c_in * Q : (c_in + 1) * Q].rearrange("p r (c i) -> p c r i", i=2),
+                op=ALU.mult,
+            )
+
+        def quant_w(k):
+            quant(w_codes[k][:], w_scales[k][:], w_bf[k][:].rearrange("p c r -> p (c r)"))
+
+        def values(k):
+            bank, slot = y_place[k]
+            nc.tensor.matmul_mx(
+                out=y_ps[bank][:, slot, :],
+                lhsT=w_codes[k][:].bitcast(FP8X4),
+                lhsT_scale=w_scales[k][:],
+                rhs=v_codes[:].bitcast(FP8X4),
+                rhs_scale=v_scales[:],
+                start=True,
+                stop=True,
+            )
+
+        def norms(b):
+            for i, k in enumerate(batches[b]):
+                bank, slot = y_place[k]
+                nc.scalar.activation(out=squares[:, k, :], in_=y_ps[bank][:, slot, :], func=ACT.Square, accum_out=ssq[b][:, i : i + 1])
+            nc.scalar.activation(out=rstd[b][:], in_=ssq[b][:], func=ACT.Abs_reciprocal_sqrt, scale=1.0 / E, bias=256.0 * EPS)
+
+        def finish(b):
+            for i, k in enumerate(batches[b]):
+                bank, slot = y_place[k]
+                nc.vector.scalar_tensor_tensor(
+                    out=o_sb[b][:, i, :], in0=y_ps[bank][:, slot, :], scalar=rstd[b][:, i : i + 1], in1=gn_sb[:], op0=ALU.mult, op1=ALU.mult
+                )
+            for i in range(0, len(batches[b]), 2):
+                h0, c0 = groups[batches[b][i]][3:]
+                h1, c1 = groups[batches[b][i + 1]][3:]
+                if h0 == h1:
+                    dst = out[h0, c0 * Q : (c0 + 2) * Q, :].rearrange("(m p) e -> p m e", p=Q)
+                else:
+                    dst = out[h0 : h1 + 1 : h1 - h0, c0 * Q : (c0 + 1) * Q, :].rearrange("h p e -> p h e")
+                nc.sync.dma_start(out=dst, in_=o_sb[b][:, i : i + 2, :])
+
+        load_k(0)
+        load_k(1)
+        load_q(0, 0)
+        nc.scalar.dma_start(out=kb_sb[:], in_=kb.rearrange("(p r) o -> p (r o)", r=PACK))
+        nc.scalar.dma_start(out=t_sb[:], in_=t.rearrange("(p r) o -> p (r o)", r=PACK))
+        load_mask(0)
+        load_q(1, 0)
+        load_q(0, 1)
+        load_q(1, 1)
+        load_mask(1)
+        load_q(0, 2)
+        load_mask(2)
+        load_q(1, 2)
+        nc.sync.dma_start(out=v_raw[:], in_=v[0].rearrange("(p r) e -> p r e", r=PACK))
+        nc.sync.dma_start(out=gn_sb[:], in_=gn)
+
+        nc.vector.memset(warm_in[:], 0.0)
+        nc.scalar.activation(out=warm_out[:], in_=warm_in[:], func=ACT.Sigmoid)
+
+        cast_k("v", 0, 0)
+        cast_k("v", 0, 1)
+        cast_k("v", 1, 0)
+        cast_k("s", 1, 1)
+        quant_k(0)
+        cast_q("s", 0, 0)
+        quant_k(1)
+        quant_q(0, 0)
+        scores(0, 0)
+        sigmoids(0, 0)
+        make_tm("v", 0)
+        cast_q("v", 1, 0)
+        quant_q(1, 0)
+        scores(1, 0)
+        sigmoids(1, 0)
+        weigh(0)
+        cast_q("v", 0, 1)
+        quant_w(0)
+        weigh(1)
+        quant_q(0, 1)
+        cast_q("v", 1, 1)
+        quant_w(1)
+        quant_q(1, 1)
+        make_tm("s", 1)
+        scores(2, 0)
+        sigmoids(2, 0)
+        scores(2, 1)
+        sigmoids(2, 1)
+        weigh(2)
+        weigh(3)
+        quant_w(2)
+        cast_q("v", 0, 2)
+        quant_w(3)
+        quant_q(0, 2)
+        make_tm("s", 2)
+        scores(3, 0)
+        sigmoids(3, 0)
+        scores(3, 1)
+        sigmoids(3, 1)
+        interleave("v", v_bf[:], v_raw[:])
+        weigh(4)
+        quant(v_codes[:], v_scales[:], v_bf[:].rearrange("p e r -> p (e r)"))
+        weigh(5)
+        quant_w(4)
+        cast_q("v", 1, 2)
+        quant_w(5)
+        weigh(6)
+        quant_q(1, 2)
+        weigh(7)
+        quant_w(6)
+        for k in range(0, 4):
+            values(k)
+        scores(4, 0)
+        sigmoids(4, 0)
+        weigh(8)
+        quant_w(7)
+        for k in range(4, 8):
+            values(k)
+        scores(4, 1)
+        sigmoids(4, 1)
+        for k in range(9, 16):
+            weigh(k)
+            quant_w(k - 1)
+            values(k - 1)
+        quant_w(15)
+        values(15)
+        for b in range(len(batches)):
+            norms(b)
+            finish(b)

@@ -30,10 +30,10 @@ def tile_rows_a_sigmoid_kb_mask_onorm_kernel(tc, qT, kT, t, v, kb, mask, gn, out
         def sbuf(name, shape, dtype):
             return sb.tile(shape, dtype, name=name, align_bytes=64)
 
-        spans = [(0, 1), (1, 1), (2, 2)]
-        span_of = {0: 0, 1: 1, 2: 2, 3: 2}
+        spans = [(0, 2), (2, 2)]
+        span_of = {0: 0, 1: 0, 2: 1, 3: 1}
 
-        k_raw = [sbuf("k_raw%d" % i, [P, PACK, N // 2], F32) for i in range(2)]
+        k_raw = sbuf("k_raw", [P, PACK, N], F32)
         k_bf = [sbuf("k_bf%d" % i, [P, 2, P, PACK], BF16) for i in range(2)]
         k_codes = [sbuf("k_codes%d" % i, [P, 2 * P], U32) for i in range(2)]
         k_scales = [sbuf("k_scales%d" % i, [P, 2 * P], U8) for i in range(2)]
@@ -57,28 +57,16 @@ def tile_rows_a_sigmoid_kb_mask_onorm_kernel(tc, qT, kT, t, v, kb, mask, gn, out
         warm_in = sbuf("warm_in", [P, 1], F32)
         warm_out = sbuf("warm_out", [P, 1], F32)
 
-        units = [[(0, 0)], [(1, 0)], [(0, 1), (1, 1)], [(0, 2), (0, 3)], [(1, 2), (1, 3)]]
-        groups = []
-        for u, members in enumerate(units):
-            for g in range(2):
-                for m, (pair, c) in enumerate(members):
-                    groups.append((u, g, m, 2 * pair + g, c))
-        p_sb = {}
-        for u, members in enumerate(units):
-            for g in range(2):
-                p_sb[u, g] = sbuf("p%d%d" % (u, g), [P, PACK, len(members) * Q], F32)
-        w_bf = [sbuf("w_bf%d" % k, [P, Q, PACK], BF16) for k in range(16)]
-        w_codes = [sbuf("w_codes%d" % k, [P, Q], U32) for k in range(16)]
-        w_scales = [sbuf("w_scales%d" % k, [P, Q], U8) for k in range(16)]
+        units = [[(0, 0), (0, 1)], [(1, 0), (1, 1)], [(0, 2), (0, 3)], [(1, 2), (1, 3)]]
+        blocks = [(0, 0), (1, 0), (2, 0), (3, 0), (0, 1), (1, 1), (2, 1), (3, 1)]
+        p_sb = [sbuf("p%d" % b, [P, PACK, 2 * Q], F32) for b in range(8)]
+        w_bf = [sbuf("w_bf%d" % b, [P, 2 * Q, PACK], BF16) for b in range(8)]
+        w_codes = [sbuf("w_codes%d" % b, [P, 2 * Q], U32) for b in range(8)]
+        w_scales = [sbuf("w_scales%d" % b, [P, 2 * Q], U8) for b in range(8)]
         squares = sbuf("squares", [P, 16, E], BF16)
-        batches = [[0, 1, 2, 3], [4, 5, 6, 7], [8, 9], [10, 11], [12, 13], [14, 15]]
-        y_place = {}
-        for b, (bank, slot) in enumerate([(0, 0), (1, 0), (2, 0), (3, 0), (2, 2), (3, 2)]):
-            for i, k in enumerate(batches[b]):
-                y_place[k] = (bank, slot + i)
-        ssq = [sbuf("ssq%d" % b, [P, len(ks)], F32) for b, ks in enumerate(batches)]
-        rstd = [sbuf("rstd%d" % b, [P, len(ks)], F32) for b, ks in enumerate(batches)]
-        o_sb = [sbuf("o%d" % b, [P, len(ks), E], F32) for b, ks in enumerate(batches)]
+        ssq = [sbuf("ssq%d" % b, [P, 4], F32) for b in range(4)]
+        rstd = [sbuf("rstd%d" % b, [P, 4], F32) for b in range(4)]
+        o_sb = [sbuf("o%d" % b, [P, 2, E], F32) for b in range(8)]
 
         s_ps = {}
         for g in range(2):
@@ -88,10 +76,9 @@ def tile_rows_a_sigmoid_kb_mask_onorm_kernel(tc, qT, kT, t, v, kb, mask, gn, out
 
         k_view = kT[0].rearrange("(p j) n -> p j n", j=PACK)
 
-        def load_k(half):
-            cols = slice(half * N // 2, (half + 1) * N // 2)
-            nc.sync.dma_start(out=k_raw[half][0:ROWS], in_=k_view[:, :, cols])
-            nc.scalar.dma_start(out=k_raw[half][ROWS:P], in_=k_view[:, :, cols])
+        def load_k():
+            nc.sync.dma_start(out=k_raw[0:ROWS], in_=k_view)
+            nc.scalar.dma_start(out=k_raw[ROWS:P], in_=k_view)
 
         def load_q(pair, s):
             c0, nch = spans[s]
@@ -109,9 +96,9 @@ def tile_rows_a_sigmoid_kb_mask_onorm_kernel(tc, qT, kT, t, v, kb, mask, gn, out
             else:
                 nc.scalar.copy(out=dst, in_=src)
 
-        def cast_k(eng, half, i):
-            src = k_raw[half][:].rearrange("p j (s r) -> p s j r", r=PACK)[:, :, :, 2 * i : 2 * i + 2]
-            dst = k_bf[i][:, :, half * ROWS : (half + 1) * ROWS, :].rearrange("p r s j -> p s j r")
+        def cast_k(eng, i, s0=0, s1=P):
+            src = k_raw[:].rearrange("p j (s r) -> p s j r", r=PACK)[:, s0:s1, :, 2 * i : 2 * i + 2]
+            dst = k_bf[i][:, :, s0:s1, :].rearrange("p r s j -> p s j r")
             cast(eng, dst, src)
 
         def interleave(eng, dst, src):
@@ -123,18 +110,22 @@ def tile_rows_a_sigmoid_kb_mask_onorm_kernel(tc, qT, kT, t, v, kb, mask, gn, out
         def quant_k(i):
             quant(k_codes[i][:], k_scales[i][:], k_bf[i][:].rearrange("p r s j -> p (r s j)"))
 
-        def cast_q(eng, pair, s):
-            interleave(eng, q_bf[pair, s][:], q_raw[pair, s][:])
+        def cast_q(eng, pair, s, a=0, b=Q):
+            src = q_raw[pair, s][:].rearrange("p j (c m) -> p c j m", m=2)[:, a:b]
+            dst = q_bf[pair, s][:].rearrange("p (m c) j -> p c j m", m=2)[:, a:b]
+            cast(eng, dst, src)
 
-        def quant_q(pair, s):
-            quant(q_codes[pair, s][:], q_scales[pair, s][:], q_bf[pair, s][:].rearrange("p c j -> p (c j)"))
+        def quant_q(pair, s, a=0, b=2 * Q):
+            quant(q_codes[pair, s][:, a:b], q_scales[pair, s][:, a:b], q_bf[pair, s][:, a:b, :].rearrange("p c j -> p (c j)"))
 
-        def make_tm(eng, s):
-            for r in range(PACK):
+        def make_tm(eng, s, rs=range(PACK)):
+            for r in rs:
+                src = m_raw[s][:, r, :].rearrange("p (c m) -> p m c", m=2)
+                dst = tm[s][:, r, :].rearrange("p (m c) -> p m c", m=2)
                 if eng == "v":
-                    nc.vector.tensor_scalar(out=tm[s][:, r, :], in0=m_raw[s][:, r, :], scalar1=t_sb[:, r : r + 1], scalar2=None, op0=ALU.mult)
+                    nc.vector.tensor_scalar(out=dst, in0=src, scalar1=t_sb[:, r : r + 1], scalar2=None, op0=ALU.mult)
                 else:
-                    nc.scalar.activation(out=tm[s][:, r, :], in_=m_raw[s][:, r, :], func=ACT.Copy, scale=t_sb[:, r : r + 1])
+                    nc.scalar.activation(out=dst, in_=src, func=ACT.Copy, scale=t_sb[:, r : r + 1])
 
         def fills(u):
             if len(units[u]) == 1:
@@ -161,150 +152,144 @@ def tile_rows_a_sigmoid_kb_mask_onorm_kernel(tc, qT, kT, t, v, kb, mask, gn, out
                             stop=True,
                         )
 
-        def sigmoids(u, f):
+        def sigmoids(u, f, gs=range(2)):
             bank, rs = fills(u)[f]
             width = len(units[u]) * Q
-            for g in range(2):
+            pair, c = units[u][0]
+            for g in gs:
                 for i, r in enumerate(rs):
                     nc.scalar.activation(
-                        out=p_sb[u, g][:, r, :],
+                        out=p_sb[blocks.index((2 * pair + g, c // 2))][:, r, (c % 2) * Q : (c % 2) * Q + width],
                         in_=s_ps[g, bank][:, i * width : (i + 1) * width],
                         func=ACT.Sigmoid,
                         bias=kb_sb[:, r : r + 1],
                     )
 
-        def weigh(k):
-            u, g, m, h, c = groups[k]
-            s = span_of[c]
-            c_in = c - spans[s][0]
+        def weigh(b, a=0, z=2 * Q):
+            s = blocks[b][1]
             nc.vector.tensor_tensor(
-                out=w_bf[k][:].rearrange("p (c i) r -> p c r i", i=2),
-                in0=p_sb[u, g][:, :, m * Q : (m + 1) * Q].rearrange("p r (c i) -> p c r i", i=2),
-                in1=tm[s][:, :, c_in * Q : (c_in + 1) * Q].rearrange("p r (c i) -> p c r i", i=2),
+                out=w_bf[b][:, a:z, :].rearrange("p (c i) r -> p c r i", i=2),
+                in0=p_sb[b][:, :, a:z].rearrange("p r (c i) -> p c r i", i=2),
+                in1=tm[s][:, :, a:z].rearrange("p r (c i) -> p c r i", i=2),
                 op=ALU.mult,
             )
 
-        def quant_w(k):
-            quant(w_codes[k][:], w_scales[k][:], w_bf[k][:].rearrange("p c r -> p (c r)"))
+        def quant_w(b, a=0, z=2 * Q):
+            quant(w_codes[b][:, a:z], w_scales[b][:, a:z], w_bf[b][:, a:z, :].rearrange("p c r -> p (c r)"))
 
-        def values(k):
-            bank, slot = y_place[k]
-            nc.tensor.matmul_mx(
-                out=y_ps[bank][:, slot, :],
-                lhsT=w_codes[k][:].bitcast(FP8X4),
-                lhsT_scale=w_scales[k][:],
-                rhs=v_codes[:].bitcast(FP8X4),
-                rhs_scale=v_scales[:],
-                start=True,
-                stop=True,
-            )
+        def values(b, ms=range(2)):
+            for m in ms:
+                nc.tensor.matmul_mx(
+                    out=y_ps[b // 2][:, 2 * (b % 2) + m, :],
+                    lhsT=w_codes[b][:, m * Q : (m + 1) * Q].bitcast(FP8X4),
+                    lhsT_scale=w_scales[b][:, m * Q : (m + 1) * Q],
+                    rhs=v_codes[:].bitcast(FP8X4),
+                    rhs_scale=v_scales[:],
+                    start=True,
+                    stop=True,
+                )
 
-        def norms(b):
-            for i, k in enumerate(batches[b]):
-                bank, slot = y_place[k]
-                nc.scalar.activation(out=squares[:, k, :], in_=y_ps[bank][:, slot, :], func=ACT.Square, accum_out=ssq[b][:, i : i + 1])
-            nc.scalar.activation(out=rstd[b][:], in_=ssq[b][:], func=ACT.Abs_reciprocal_sqrt, scale=1.0 / E, bias=256.0 * EPS)
+        def sums(bank, slots=range(4)):
+            for i in slots:
+                nc.scalar.activation(out=squares[:, 4 * bank + i, :], in_=y_ps[bank][:, i, :], func=ACT.Square, accum_out=ssq[bank][:, i : i + 1])
+
+        def norms(bank, a=0, z=4):
+            nc.scalar.activation(out=rstd[bank][:, a:z], in_=ssq[bank][:, a:z], func=ACT.Abs_reciprocal_sqrt, scale=1.0 / E, bias=256.0 * EPS)
 
         def finish(b):
-            for i, k in enumerate(batches[b]):
-                bank, slot = y_place[k]
+            bank = b // 2
+            for m in range(2):
+                i = 2 * (b % 2) + m
                 nc.vector.scalar_tensor_tensor(
-                    out=o_sb[b][:, i, :], in0=y_ps[bank][:, slot, :], scalar=rstd[b][:, i : i + 1], in1=gn_sb[:], op0=ALU.mult, op1=ALU.mult
+                    out=o_sb[b][:, m, :], in0=y_ps[bank][:, i, :], scalar=rstd[bank][:, i : i + 1], in1=gn_sb[:], op0=ALU.mult, op1=ALU.mult
                 )
-            for i in range(0, len(batches[b]), 2):
-                h0, c0 = groups[batches[b][i]][3:]
-                h1, c1 = groups[batches[b][i + 1]][3:]
-                if h0 == h1:
-                    dst = out[h0, c0 * Q : (c0 + 2) * Q, :].rearrange("(m p) e -> p m e", p=Q)
-                else:
-                    dst = out[h0 : h1 + 1 : h1 - h0, c0 * Q : (c0 + 1) * Q, :].rearrange("h p e -> p h e")
-                nc.sync.dma_start(out=dst, in_=o_sb[b][:, i : i + 2, :])
+            h, s = blocks[b]
+            dst = out[h, s * 2 * Q : (s + 1) * 2 * Q, :].rearrange("(p m) e -> p m e", m=2)
+            nc.sync.dma_start(out=dst, in_=o_sb[b][:])
 
-        load_k(0)
-        load_k(1)
+
+        load_k()
         load_q(0, 0)
         nc.scalar.dma_start(out=kb_sb[:], in_=kb.rearrange("(p r) o -> p (r o)", r=PACK))
         nc.scalar.dma_start(out=t_sb[:], in_=t.rearrange("(p r) o -> p (r o)", r=PACK))
-        load_mask(0)
         load_q(1, 0)
+        load_mask(0)
         load_q(0, 1)
         load_q(1, 1)
         load_mask(1)
-        load_q(0, 2)
-        load_mask(2)
-        load_q(1, 2)
         nc.sync.dma_start(out=v_raw[:], in_=v[0].rearrange("(p r) e -> p r e", r=PACK))
         nc.sync.dma_start(out=gn_sb[:], in_=gn)
-
         nc.vector.memset(warm_in[:], 0.0)
         nc.scalar.activation(out=warm_out[:], in_=warm_in[:], func=ACT.Sigmoid)
-
-        cast_k("v", 0, 0)
-        cast_k("v", 0, 1)
-        cast_k("v", 1, 0)
-        cast_k("s", 1, 1)
+        cast_k("v", 0)
+        cast_k("s", 1, 0, 64)
+        cast_k("v", 1, 64, 128)
         quant_k(0)
-        cast_q("s", 0, 0)
         quant_k(1)
+        cast_q("v", 0, 0, 0, 80)
+        cast_q("s", 0, 0, 80, Q)
         quant_q(0, 0)
         scores(0, 0)
-        sigmoids(0, 0)
-        make_tm("v", 0)
+        scores(0, 1)
+        sigmoids(0, 0, [0])
+        sigmoids(0, 1, [0])
+        sigmoids(0, 0, [1])
+        sigmoids(0, 1, [1])
         cast_q("v", 1, 0)
         quant_q(1, 0)
         scores(1, 0)
         sigmoids(1, 0)
-        weigh(0)
+        scores(1, 1)
+        sigmoids(1, 1)
+        make_tm("v", 0)
+        weigh(0, 0, Q)
         cast_q("v", 0, 1)
-        quant_w(0)
-        weigh(1)
+        weigh(0, Q, 2 * Q)
         quant_q(0, 1)
+        weigh(1, 0, Q)
         cast_q("v", 1, 1)
-        quant_w(1)
+        weigh(1, Q, 2 * Q)
         quant_q(1, 1)
-        make_tm("s", 1)
         scores(2, 0)
         sigmoids(2, 0)
         scores(2, 1)
+        make_tm("s", 1)
         sigmoids(2, 1)
-        weigh(2)
-        weigh(3)
-        quant_w(2)
-        cast_q("v", 0, 2)
-        quant_w(3)
-        quant_q(0, 2)
-        make_tm("s", 2)
         scores(3, 0)
+        interleave("s", v_bf[:], v_raw[:])
         sigmoids(3, 0)
         scores(3, 1)
         sigmoids(3, 1)
-        interleave("v", v_bf[:], v_raw[:])
+        quant_w(0)
+        weigh(2)
+        quant_w(1)
+        weigh(3)
+        quant_w(2)
         weigh(4)
         quant(v_codes[:], v_scales[:], v_bf[:].rearrange("p e r -> p (e r)"))
-        weigh(5)
-        quant_w(4)
-        cast_q("v", 1, 2)
-        quant_w(5)
-        weigh(6)
-        quant_q(1, 2)
-        weigh(7)
-        quant_w(6)
-        for k in range(0, 4):
-            values(k)
-        scores(4, 0)
-        sigmoids(4, 0)
-        weigh(8)
+        quant_w(3)
+        for b in range(0, 4):
+            values(b)
+        for b in range(5, 8):
+            weigh(b)
+            quant_w(b - 1)
+            values(b - 1)
+        sums(0)
+        norms(0)
+        sums(1)
+        finish(0)
         quant_w(7)
-        for k in range(4, 8):
-            values(k)
-        scores(4, 1)
-        sigmoids(4, 1)
-        for k in range(9, 16):
-            weigh(k)
-            quant_w(k - 1)
-            values(k - 1)
-        quant_w(15)
-        values(15)
-        for b in range(len(batches)):
-            norms(b)
-            finish(b)
+        sums(2, [0])
+        norms(1)
+        sums(2, [1, 2, 3])
+        values(7)
+        finish(1)
+        finish(2)
+        finish(3)
+        norms(2)
+        sums(3)
+        finish(4)
+        finish(5)
+        norms(3)
+        finish(6)
+        finish(7)

@@ -9,6 +9,7 @@ F32 = mybir.dt.float32
 BF16 = mybir.dt.bfloat16
 U32 = mybir.dt.uint32
 U8 = mybir.dt.uint8
+I32 = mybir.dt.int32
 FP8X4 = mybir.dt.float8_e4m3fn_x4
 ACT = mybir.ActivationFunctionType
 ALU = mybir.AluOpType
@@ -33,10 +34,10 @@ def tile_rows_a_sigmoid_kb_mask_onorm_kernel(tc, qT, kT, t, v, kb, mask, gn, out
         spans = [(0, 2), (2, 2)]
         span_of = {0: 0, 1: 0, 2: 1, 3: 1}
 
-        k_raw = sbuf("k_raw", [P, PACK, N], F32)
-        k_bf = [sbuf("k_bf%d" % i, [P, 2, P, PACK], BF16) for i in range(2)]
-        k_codes = [sbuf("k_codes%d" % i, [P, 2 * P], U32) for i in range(2)]
-        k_scales = [sbuf("k_scales%d" % i, [P, 2 * P], U8) for i in range(2)]
+        k_raw = sbuf("k_raw", [P, PACK, N // 2], F32)
+        k_bf = sbuf("k_bf", [P, PACK, ROWS, PACK], BF16)
+        k_codes = sbuf("k_codes", [P, PACK, 3 * ROWS], I32)
+        k_scales = sbuf("k_scales", [P, PACK, 3 * ROWS], U8)
         q_raw, q_bf, q_codes, q_scales = {}, {}, {}, {}
         for pair in range(2):
             for s, (c0, nch) in enumerate(spans):
@@ -64,8 +65,9 @@ def tile_rows_a_sigmoid_kb_mask_onorm_kernel(tc, qT, kT, t, v, kb, mask, gn, out
         w_codes = [sbuf("w_codes%d" % b, [P, 2 * Q], U32) for b in range(8)]
         w_scales = [sbuf("w_scales%d" % b, [P, 2 * Q], U8) for b in range(8)]
         squares = sbuf("squares", [P, 16, E], BF16)
-        ssq = [sbuf("ssq%d" % b, [P, 4], F32) for b in range(4)]
-        rstd = [sbuf("rstd%d" % b, [P, 4], F32) for b in range(4)]
+        ssq = sbuf("ssq", [P, 16], F32)
+        rstd = sbuf("rstd", [P, 16], F32)
+        y_place = [(0, 0), (0, 2), (1, 0), (1, 2), (2, 0), (3, 0), (2, 2), (3, 2)]
         o_sb = [sbuf("o%d" % b, [P, 2, E], F32) for b in range(8)]
 
         s_ps = {}
@@ -77,8 +79,16 @@ def tile_rows_a_sigmoid_kb_mask_onorm_kernel(tc, qT, kT, t, v, kb, mask, gn, out
         k_view = kT[0].rearrange("(p j) n -> p j n", j=PACK)
 
         def load_k():
-            nc.sync.dma_start(out=k_raw[0:ROWS], in_=k_view)
-            nc.scalar.dma_start(out=k_raw[ROWS:P], in_=k_view)
+            nc.sync.dma_start(out=k_raw[0:ROWS], in_=k_view[:, :, 0 : N // 2])
+            nc.scalar.dma_start(out=k_raw[ROWS:P], in_=k_view[:, :, N // 2 : N])
+
+        def swap_k():
+            words = ROWS // 4
+            scale_words = k_scales[:].bitcast(I32)
+            nc.scalar.dma_start(out=k_codes[0:ROWS, :, 2 * ROWS : 3 * ROWS], in_=k_codes[ROWS:P, :, ROWS : 2 * ROWS])
+            nc.scalar.dma_start(out=k_codes[ROWS:P, :, 0:ROWS], in_=k_codes[0:ROWS, :, ROWS : 2 * ROWS])
+            nc.scalar.dma_start(out=scale_words[0:ROWS, :, 2 * words : 3 * words], in_=scale_words[ROWS:P, :, words : 2 * words])
+            nc.scalar.dma_start(out=scale_words[ROWS:P, :, 0:words], in_=scale_words[0:ROWS, :, words : 2 * words])
 
         def load_q(pair, s):
             c0, nch = spans[s]
@@ -96,9 +106,9 @@ def tile_rows_a_sigmoid_kb_mask_onorm_kernel(tc, qT, kT, t, v, kb, mask, gn, out
             else:
                 nc.scalar.copy(out=dst, in_=src)
 
-        def cast_k(eng, i, s0=0, s1=P):
-            src = k_raw[:].rearrange("p j (s r) -> p s j r", r=PACK)[:, s0:s1, :, 2 * i : 2 * i + 2]
-            dst = k_bf[i][:, :, s0:s1, :].rearrange("p r s j -> p s j r")
+        def cast_k(eng, s0, s1):
+            src = k_raw[:].rearrange("p j (s r) -> p s j r", r=PACK)[:, s0:s1]
+            dst = k_bf[:, :, s0:s1, :].rearrange("p r s j -> p s j r")
             cast(eng, dst, src)
 
         def interleave(eng, dst, src):
@@ -107,8 +117,8 @@ def tile_rows_a_sigmoid_kb_mask_onorm_kernel(tc, qT, kT, t, v, kb, mask, gn, out
         def quant(codes, scales, src):
             nc.vector.quantize_mx(out=codes.bitcast(FP8X4), scales=scales, in_=src)
 
-        def quant_k(i):
-            quant(k_codes[i][:], k_scales[i][:], k_bf[i][:].rearrange("p r s j -> p (r s j)"))
+        def quant_k(r):
+            quant(k_codes[:, r, ROWS : 2 * ROWS], k_scales[:, r, ROWS : 2 * ROWS], k_bf[:, r].rearrange("p s j -> p (s j)"))
 
         def cast_q(eng, pair, s, a=0, b=Q):
             src = q_raw[pair, s][:].rearrange("p j (c m) -> p c j m", m=2)[:, a:b]
@@ -127,43 +137,42 @@ def tile_rows_a_sigmoid_kb_mask_onorm_kernel(tc, qT, kT, t, v, kb, mask, gn, out
                 else:
                     nc.scalar.activation(out=dst, in_=src, func=ACT.Copy, scale=t_sb[:, r : r + 1])
 
-        def fills(u):
-            if len(units[u]) == 1:
-                return [(u % 2, [0, 1, 2, 3])]
-            return [(0, [0, 1]), (1, [2, 3])]
+        def score(n, j):
+            u, i, g = n // 4, (n // 2) % 2, n % 2
+            r, m = (j, i) if u == 0 else (2 * i + j // 2, j % 2)
+            pair, s = u % 2, u // 2
+            rows = slice(g * ROWS, (g + 1) * ROWS)
+            kcols = slice((1 - g) * ROWS, (1 - g) * ROWS + P)
+            qcols = slice(m * Q, (m + 1) * Q)
+            nc.tensor.matmul_mx(
+                out=s_ps[g, i][:, j * Q : (j + 1) * Q],
+                lhsT=k_codes[rows, r, kcols].bitcast(FP8X4),
+                lhsT_scale=k_scales[rows, r, kcols],
+                rhs=q_codes[pair, s][rows, qcols].bitcast(FP8X4),
+                rhs_scale=q_scales[pair, s][rows, qcols],
+                start=True,
+                stop=True,
+            )
 
-        def scores(u, f):
-            bank, rs = fills(u)[f]
-            width = len(units[u]) * Q
-            for i, r in enumerate(rs):
-                for m, (pair, c) in enumerate(units[u]):
-                    s = span_of[c]
-                    qcols = slice((c - spans[s][0]) * Q, (c - spans[s][0] + 1) * Q)
-                    kcols = slice((r % 2) * P, (r % 2 + 1) * P)
-                    for g in range(2):
-                        rows = slice(g * ROWS, (g + 1) * ROWS)
-                        nc.tensor.matmul_mx(
-                            out=s_ps[g, bank][:, i * width + m * Q : i * width + (m + 1) * Q],
-                            lhsT=k_codes[r // 2][rows, kcols].bitcast(FP8X4),
-                            lhsT_scale=k_scales[r // 2][rows, kcols],
-                            rhs=q_codes[pair, s][rows, qcols].bitcast(FP8X4),
-                            rhs_scale=q_scales[pair, s][rows, qcols],
-                            start=True,
-                            stop=True,
-                        )
+        def scores(n):
+            for j in range(2):
+                work = [(n - 1, 2 + j), (n, j)]
+                for fill, part in work if n % 2 else reversed(work):
+                    if 0 <= fill < 16:
+                        score(fill, part)
 
-        def sigmoids(u, f, gs=range(2)):
-            bank, rs = fills(u)[f]
-            width = len(units[u]) * Q
-            pair, c = units[u][0]
-            for g in gs:
-                for i, r in enumerate(rs):
-                    nc.scalar.activation(
-                        out=p_sb[blocks.index((2 * pair + g, c // 2))][:, r, (c % 2) * Q : (c % 2) * Q + width],
-                        in_=s_ps[g, bank][:, i * width : (i + 1) * width],
-                        func=ACT.Sigmoid,
-                        bias=kb_sb[:, r : r + 1],
-                    )
+        def sigmoids(n):
+            u, i, g = n // 4, (n // 2) % 2, n % 2
+            count = 4 if u == 0 else 2
+            width = 4 * Q // count
+            for j in range(count):
+                r, a = (j, i * Q) if u == 0 else (2 * i + j, 0)
+                nc.scalar.activation(
+                    out=p_sb[2 * u + g][:, r, a : a + width],
+                    in_=s_ps[g, i][:, j * width : (j + 1) * width],
+                    func=ACT.Sigmoid,
+                    bias=kb_sb[:, r : r + 1],
+                )
 
         def weigh(b, a=0, z=2 * Q):
             s = blocks[b][1]
@@ -180,7 +189,7 @@ def tile_rows_a_sigmoid_kb_mask_onorm_kernel(tc, qT, kT, t, v, kb, mask, gn, out
         def values(b, ms=range(2)):
             for m in ms:
                 nc.tensor.matmul_mx(
-                    out=y_ps[b // 2][:, 2 * (b % 2) + m, :],
+                    out=y_ps[y_place[b][0]][:, y_place[b][1] + m, :],
                     lhsT=w_codes[b][:, m * Q : (m + 1) * Q].bitcast(FP8X4),
                     lhsT_scale=w_scales[b][:, m * Q : (m + 1) * Q],
                     rhs=v_codes[:].bitcast(FP8X4),
@@ -189,19 +198,19 @@ def tile_rows_a_sigmoid_kb_mask_onorm_kernel(tc, qT, kT, t, v, kb, mask, gn, out
                     stop=True,
                 )
 
-        def sums(bank, slots=range(4)):
-            for i in slots:
-                nc.scalar.activation(out=squares[:, 4 * bank + i, :], in_=y_ps[bank][:, i, :], func=ACT.Square, accum_out=ssq[bank][:, i : i + 1])
+        def sums(b):
+            bank, slot = y_place[b]
+            for m in range(2):
+                nc.scalar.activation(out=squares[:, 2 * b + m, :], in_=y_ps[bank][:, slot + m, :], func=ACT.Square, accum_out=ssq[:, 2 * b + m : 2 * b + m + 1])
 
-        def norms(bank, a=0, z=4):
-            nc.scalar.activation(out=rstd[bank][:, a:z], in_=ssq[bank][:, a:z], func=ACT.Abs_reciprocal_sqrt, scale=1.0 / E, bias=256.0 * EPS)
+        def norms(a, z):
+            nc.scalar.activation(out=rstd[:, 2 * a : 2 * z], in_=ssq[:, 2 * a : 2 * z], func=ACT.Abs_reciprocal_sqrt, scale=1.0 / E, bias=256.0 * EPS)
 
         def finish(b):
-            bank = b // 2
+            bank, slot = y_place[b]
             for m in range(2):
-                i = 2 * (b % 2) + m
                 nc.vector.scalar_tensor_tensor(
-                    out=o_sb[b][:, m, :], in0=y_ps[bank][:, i, :], scalar=rstd[bank][:, i : i + 1], in1=gn_sb[:], op0=ALU.mult, op1=ALU.mult
+                    out=o_sb[b][:, m, :], in0=y_ps[bank][:, slot + m, :], scalar=rstd[:, 2 * b + m : 2 * b + m + 1], in1=gn_sb[:], op0=ALU.mult, op1=ALU.mult
                 )
             h, s = blocks[b]
             dst = out[h, s * 2 * Q : (s + 1) * 2 * Q, :].rearrange("(p m) e -> p m e", m=2)
@@ -215,81 +224,94 @@ def tile_rows_a_sigmoid_kb_mask_onorm_kernel(tc, qT, kT, t, v, kb, mask, gn, out
         load_q(1, 0)
         load_mask(0)
         load_q(0, 1)
-        load_q(1, 1)
-        load_mask(1)
-        nc.sync.dma_start(out=v_raw[:], in_=v[0].rearrange("(p r) e -> p r e", r=PACK))
-        nc.sync.dma_start(out=gn_sb[:], in_=gn)
         nc.vector.memset(warm_in[:], 0.0)
+        nc.vector.memset(k_scales[:].bitcast(I32), 0)
         nc.scalar.activation(out=warm_out[:], in_=warm_in[:], func=ACT.Sigmoid)
-        cast_k("v", 0)
-        cast_k("s", 1, 0, 64)
-        cast_k("v", 1, 64, 128)
+        cast_k("v", 0, 40)
+        cast_k("s", 40, 64)
         quant_k(0)
         quant_k(1)
-        cast_q("v", 0, 0, 0, 80)
-        cast_q("s", 0, 0, 80, Q)
+        quant_k(2)
+        quant_k(3)
+        swap_k()
+        load_q(1, 1)
+        nc.sync.dma_start(out=v_raw[:], in_=v[0].rearrange("(p r) e -> p r e", r=PACK))
+        load_mask(1)
+        nc.sync.dma_start(out=gn_sb[:], in_=gn)
+        cast_q("v", 0, 0)
         quant_q(0, 0)
-        scores(0, 0)
-        scores(0, 1)
-        sigmoids(0, 0, [0])
-        sigmoids(0, 1, [0])
-        sigmoids(0, 0, [1])
-        sigmoids(0, 1, [1])
         cast_q("v", 1, 0)
         quant_q(1, 0)
-        scores(1, 0)
-        sigmoids(1, 0)
-        scores(1, 1)
-        sigmoids(1, 1)
         make_tm("v", 0)
+        scores(0)
+        scores(1)
+        scores(2)
+        scores(3)
+        sigmoids(0)
+        scores(4)
+        sigmoids(1)
+        scores(5)
+        sigmoids(2)
+        scores(6)
+        sigmoids(3)
+        scores(7)
         weigh(0, 0, Q)
         cast_q("v", 0, 1)
-        weigh(0, Q, 2 * Q)
-        quant_q(0, 1)
         weigh(1, 0, Q)
+        quant_q(0, 1)
+        weigh(0, Q, 2 * Q)
         cast_q("v", 1, 1)
         weigh(1, Q, 2 * Q)
         quant_q(1, 1)
-        scores(2, 0)
-        sigmoids(2, 0)
-        scores(2, 1)
-        make_tm("s", 1)
-        sigmoids(2, 1)
-        scores(3, 0)
-        interleave("s", v_bf[:], v_raw[:])
-        sigmoids(3, 0)
-        scores(3, 1)
-        sigmoids(3, 1)
+        interleave("v", v_bf[:], v_raw[:])
         quant_w(0)
+        quant(v_codes[:], v_scales[:], v_bf[:].rearrange("p e r -> p (e r)"))
+        for n in range(4, 10):
+            sigmoids(n)
+            scores(n + 4)
         weigh(2)
         quant_w(1)
+        make_tm("v", 1, [0, 1])
+        make_tm("s", 1, [2, 3])
+        values(0)
+        sigmoids(10)
+        scores(14)
+        values(1)
+        sigmoids(11)
+        scores(15)
+        scores(16)
         weigh(3)
         quant_w(2)
         weigh(4)
-        quant(v_codes[:], v_scales[:], v_bf[:].rearrange("p e r -> p (e r)"))
         quant_w(3)
-        for b in range(0, 4):
-            values(b)
-        for b in range(5, 8):
-            weigh(b)
-            quant_w(b - 1)
-            values(b - 1)
+        values(2)
+        values(3)
+        sigmoids(12)
+        sigmoids(13)
         sums(0)
-        norms(0)
+        sigmoids(14)
         sums(1)
+        sigmoids(15)
+        sums(2)
+        norms(0, 3)
+        weigh(5)
+        quant_w(4)
+        values(4)
+        weigh(6)
+        quant_w(5)
+        values(5)
+        sums(3)
+        sums(4)
+        weigh(7)
+        quant_w(6)
+        values(6)
+        sums(5)
         finish(0)
         quant_w(7)
-        sums(2, [0])
-        norms(1)
-        sums(2, [1, 2, 3])
         values(7)
-        finish(1)
-        finish(2)
-        finish(3)
-        norms(2)
-        sums(3)
-        finish(4)
-        finish(5)
-        norms(3)
-        finish(6)
-        finish(7)
+        norms(3, 6)
+        sums(6)
+        sums(7)
+        norms(6, 8)
+        for b in range(1, 8):
+            finish(b)

@@ -67,7 +67,7 @@ def tile_rows_a_sigmoid_kb_mask_onorm_kernel(tc, qT, kT, t, v, kb, mask, gn, out
         squares = sbuf("squares", [P, 16, E], BF16)
         ssq = sbuf("ssq", [P, 16], F32)
         rstd = sbuf("rstd", [P, 16], F32)
-        y_place = [(0, 0), (0, 2), (1, 0), (1, 2), (2, 0), (3, 0), (2, 2), (3, 2)]
+        y_place = [(0, 0), (1, 0), (2, 0), (3, 0), (2, 2), (3, 2), (0, 2), (1, 2)]
         o_sb = [sbuf("o%d" % b, [P, 2, E], F32) for b in range(8)]
 
         s_ps = {}
@@ -85,10 +85,10 @@ def tile_rows_a_sigmoid_kb_mask_onorm_kernel(tc, qT, kT, t, v, kb, mask, gn, out
         def swap_k():
             words = ROWS // 4
             scale_words = k_scales[:].bitcast(I32)
-            nc.scalar.dma_start(out=k_codes[0:ROWS, :, 2 * ROWS : 3 * ROWS], in_=k_codes[ROWS:P, :, ROWS : 2 * ROWS])
-            nc.scalar.dma_start(out=k_codes[ROWS:P, :, 0:ROWS], in_=k_codes[0:ROWS, :, ROWS : 2 * ROWS])
-            nc.scalar.dma_start(out=scale_words[0:ROWS, :, 2 * words : 3 * words], in_=scale_words[ROWS:P, :, words : 2 * words])
-            nc.scalar.dma_start(out=scale_words[ROWS:P, :, 0:words], in_=scale_words[0:ROWS, :, words : 2 * words])
+            nc.sync.dma_start(out=k_codes[0:ROWS, :, 2 * ROWS : 3 * ROWS], in_=k_codes[ROWS:P, :, ROWS : 2 * ROWS])
+            nc.sync.dma_start(out=scale_words[0:ROWS, :, 2 * words : 3 * words], in_=scale_words[ROWS:P, :, words : 2 * words])
+            nc.sync.dma_start(out=k_codes[ROWS:P, :, 0:ROWS], in_=k_codes[0:ROWS, :, ROWS : 2 * ROWS])
+            nc.sync.dma_start(out=scale_words[ROWS:P, :, 0:words], in_=scale_words[0:ROWS, :, words : 2 * words])
 
         def load_q(pair, s):
             c0, nch = spans[s]
@@ -157,6 +157,8 @@ def tile_rows_a_sigmoid_kb_mask_onorm_kernel(tc, qT, kT, t, v, kb, mask, gn, out
         def scores(n):
             for j in range(2):
                 work = [(n - 1, 2 + j), (n, j)]
+                if n == 1:
+                    work = [(j, 2 - 2 * j), (j, 3 - 2 * j)]
                 for fill, part in work if n % 2 else reversed(work):
                     if 0 <= fill < 16:
                         score(fill, part)
@@ -222,8 +224,6 @@ def tile_rows_a_sigmoid_kb_mask_onorm_kernel(tc, qT, kT, t, v, kb, mask, gn, out
         nc.scalar.dma_start(out=kb_sb[:], in_=kb.rearrange("(p r) o -> p (r o)", r=PACK))
         nc.scalar.dma_start(out=t_sb[:], in_=t.rearrange("(p r) o -> p (r o)", r=PACK))
         load_q(1, 0)
-        load_mask(0)
-        load_q(0, 1)
         nc.vector.memset(warm_in[:], 0.0)
         nc.vector.memset(k_scales[:].bitcast(I32), 0)
         nc.scalar.activation(out=warm_out[:], in_=warm_in[:], func=ACT.Sigmoid)
@@ -234,6 +234,8 @@ def tile_rows_a_sigmoid_kb_mask_onorm_kernel(tc, qT, kT, t, v, kb, mask, gn, out
         quant_k(2)
         quant_k(3)
         swap_k()
+        load_mask(0)
+        load_q(0, 1)
         load_q(1, 1)
         nc.sync.dma_start(out=v_raw[:], in_=v[0].rearrange("(p r) e -> p r e", r=PACK))
         load_mask(1)
@@ -266,13 +268,22 @@ def tile_rows_a_sigmoid_kb_mask_onorm_kernel(tc, qT, kT, t, v, kb, mask, gn, out
         interleave("v", v_bf[:], v_raw[:])
         quant_w(0)
         quant(v_codes[:], v_scales[:], v_bf[:].rearrange("p e r -> p (e r)"))
-        for n in range(4, 10):
-            sigmoids(n)
-            scores(n + 4)
+        sigmoids(4)
+        scores(8)
+        sigmoids(5)
+        scores(9)
+        sigmoids(6)
+        scores(10)
+        sigmoids(7)
+        scores(11)
+        sigmoids(8)
+        scores(12)
+        sigmoids(9)
+        scores(13)
         weigh(2)
         quant_w(1)
-        make_tm("v", 1, [0, 1])
-        make_tm("s", 1, [2, 3])
+        make_tm("v", 1, [0])
+        make_tm("s", 1, [1, 2, 3])
         values(0)
         sigmoids(10)
         scores(14)
@@ -301,17 +312,24 @@ def tile_rows_a_sigmoid_kb_mask_onorm_kernel(tc, qT, kT, t, v, kb, mask, gn, out
         quant_w(5)
         values(5)
         sums(3)
-        sums(4)
         weigh(7)
         quant_w(6)
-        values(6)
+        sums(4)
         sums(5)
         finish(0)
+        values(6)
         quant_w(7)
+        finish(1)
         values(7)
-        norms(3, 6)
+        norms(3, 5)
         sums(6)
+        norms(5, 6)
         sums(7)
-        norms(6, 8)
-        for b in range(1, 8):
-            finish(b)
+        norms(6, 7)
+        norms(7, 8)
+        finish(2)
+        finish(3)
+        finish(4)
+        finish(5)
+        finish(6)
+        finish(7)

from contextlib import ExitStack

import concourse.mybir as mybir

H, D, NQ, N, E = 4, 256, 512, 512, 128
FLOPS = 2 * H * N * NQ * D + 2 * H * NQ * N * E

F32 = mybir.dt.float32
BF16 = mybir.dt.bfloat16
U32 = mybir.dt.uint32
U8 = mybir.dt.uint8
I32 = mybir.dt.int32
FP8X4 = mybir.dt.float8_e4m3fn_x4
ACT = mybir.ActivationFunctionType
ALU = mybir.AluOpType

P = 128
ROWS = 64
PACK = 4
Q = 128
EPS = 1e-5


def tile_rows_a_sigmoid_kb_mask_onorm_kernel(tc, qT, kT, t, v, kb, mask, gn, out):
    nc = tc.nc
    with ExitStack() as ctx:
        sb = ctx.enter_context(tc.tile_pool(name="sb", bufs=1))
        ps = ctx.enter_context(tc.psum_pool(name="ps", bufs=1))
        ctx.enter_context(tc.manual_schedule())

        def sbuf(name, shape, dtype):
            return sb.tile(shape, dtype, name=name, align_bytes=64)

        spans = [(0, 2), (2, 2)]
        span_of = {0: 0, 1: 0, 2: 1, 3: 1}

        k_raw = sbuf("k_raw", [P, PACK, N // 2], F32)
        k_bf = sbuf("k_bf", [P, PACK, ROWS, PACK], BF16)
        k_codes = sbuf("k_codes", [P, PACK, 3 * ROWS], I32)
        k_scales = sbuf("k_scales", [P, PACK, 3 * ROWS], U8)
        q_raw, q_bf, q_codes, q_scales = {}, {}, {}, {}
        for pair in range(2):
            for s, (c0, nch) in enumerate(spans):
                w = nch * Q
                q_raw[pair, s] = sbuf("q_raw%d%d" % (pair, s), [P, PACK, w], F32)
                q_bf[pair, s] = sbuf("q_bf%d%d" % (pair, s), [P, w, PACK], BF16)
                q_codes[pair, s] = sbuf("q_codes%d%d" % (pair, s), [P, w], U32)
                q_scales[pair, s] = sbuf("q_scales%d%d" % (pair, s), [P, w], U8)
        m_raw = [sbuf("m_raw%d" % s, [P, PACK, nch * Q], F32) for s, (c0, nch) in enumerate(spans)]
        tm = [sbuf("tm%d" % s, [P, PACK, nch * Q], F32) for s, (c0, nch) in enumerate(spans)]
        v_raw = sbuf("v_raw", [P, PACK, E], F32)
        v_bf = sbuf("v_bf", [P, E, PACK], BF16)
        v_codes = sbuf("v_codes", [P, E], U32)
        v_scales = sbuf("v_scales", [P, E], U8)
        kb_sb = sbuf("kb_sb", [P, PACK], F32)
        t_sb = sbuf("t_sb", [P, PACK], F32)
        gn_sb = sbuf("gn_sb", [P, E], F32)
        warm_in = sbuf("warm_in", [P, 1], F32)
        warm_out = sbuf("warm_out", [P, 1], F32)

        units = [[(0, 0), (0, 1)], [(1, 0), (1, 1)], [(0, 2), (0, 3)], [(1, 2), (1, 3)]]
        blocks = [(0, 0), (1, 0), (2, 0), (3, 0), (0, 1), (1, 1), (2, 1), (3, 1)]
        p_sb = [sbuf("p%d" % b, [P, PACK, 2 * Q], F32) for b in range(8)]
        w_bf = [sbuf("w_bf%d" % b, [P, 2 * Q, PACK], BF16) for b in range(8)]
        w_codes = [sbuf("w_codes%d" % b, [P, 2 * Q], U32) for b in range(8)]
        w_scales = [sbuf("w_scales%d" % b, [P, 2 * Q], U8) for b in range(8)]
        squares = sbuf("squares", [P, 16, E], BF16)
        ssq = sbuf("ssq", [P, 16], F32)
        rstd = sbuf("rstd", [P, 16], F32)
        y_place = [(0, 0), (1, 0), (2, 0), (3, 0), (2, 2), (3, 2), (0, 2), (1, 2)]
        o_sb = [sbuf("o%d" % b, [P, 2, E], F32) for b in range(8)]

        s_ps = {}
        for g in range(2):
            for i in range(2):
                s_ps[g, i] = ps.tile([P, 4 * Q], F32, name="s%d%d" % (g, i))
        y_ps = [ps.tile([P, 4, E], F32, name="y%d" % i) for i in range(4)]

        k_view = kT[0].rearrange("(p j) n -> p j n", j=PACK)

        def load_k():
            nc.sync.dma_start(out=k_raw[0:ROWS], in_=k_view[:, :, 0 : N // 2])
            nc.scalar.dma_start(out=k_raw[ROWS:P], in_=k_view[:, :, N // 2 : N])

        def swap_k():
            words = ROWS // 4
            scale_words = k_scales[:].bitcast(I32)
            nc.sync.dma_start(out=k_codes[0:ROWS, :, 2 * ROWS : 3 * ROWS], in_=k_codes[ROWS:P, :, ROWS : 2 * ROWS])
            nc.sync.dma_start(out=scale_words[0:ROWS, :, 2 * words : 3 * words], in_=scale_words[ROWS:P, :, words : 2 * words])
            nc.sync.dma_start(out=k_codes[ROWS:P, :, 0:ROWS], in_=k_codes[0:ROWS, :, ROWS : 2 * ROWS])
            nc.sync.dma_start(out=scale_words[ROWS:P, :, 0:words], in_=scale_words[0:ROWS, :, words : 2 * words])

        def load_q(pair, s):
            c0, nch = spans[s]
            src = qT[2 * pair : 2 * pair + 2].rearrange("h (p j) n -> (h p) j n", j=PACK)
            nc.sync.dma_start(out=q_raw[pair, s][:], in_=src[:, :, c0 * Q : (c0 + nch) * Q])

        def load_mask(s):
            c0, nch = spans[s]
            src = mask.rearrange("(p r) n -> p r n", r=PACK)
            nc.sync.dma_start(out=m_raw[s][:], in_=src[:, :, c0 * Q : (c0 + nch) * Q])

        def cast(eng, dst, src):
            if eng == "v":
                nc.vector.tensor_copy(out=dst, in_=src)
            else:
                nc.scalar.copy(out=dst, in_=src)

        def cast_k(eng, s0, s1):
            src = k_raw[:].rearrange("p j (s r) -> p s j r", r=PACK)[:, s0:s1]
            dst = k_bf[:, :, s0:s1, :].rearrange("p r s j -> p s j r")
            cast(eng, dst, src)

        def interleave(eng, dst, src):
            cast(eng, dst.rearrange("p (c i) j -> p c j i", i=2), src.rearrange("p j (c i) -> p c j i", i=2))

        def quant(codes, scales, src):
            nc.vector.quantize_mx(out=codes.bitcast(FP8X4), scales=scales, in_=src)

        def quant_k(r):
            quant(k_codes[:, r, ROWS : 2 * ROWS], k_scales[:, r, ROWS : 2 * ROWS], k_bf[:, r].rearrange("p s j -> p (s j)"))

        def cast_q(eng, pair, s, a=0, b=Q):
            src = q_raw[pair, s][:].rearrange("p j (c m) -> p c j m", m=2)[:, a:b]
            dst = q_bf[pair, s][:].rearrange("p (m c) j -> p c j m", m=2)[:, a:b]
            cast(eng, dst, src)

        def quant_q(pair, s, a=0, b=2 * Q):
            quant(q_codes[pair, s][:, a:b], q_scales[pair, s][:, a:b], q_bf[pair, s][:, a:b, :].rearrange("p c j -> p (c j)"))

        def make_tm(eng, s, rs=range(PACK)):
            for r in rs:
                src = m_raw[s][:, r, :].rearrange("p (c m) -> p m c", m=2)
                dst = tm[s][:, r, :].rearrange("p (m c) -> p m c", m=2)
                if eng == "v":
                    nc.vector.tensor_scalar(out=dst, in0=src, scalar1=t_sb[:, r : r + 1], scalar2=None, op0=ALU.mult)
                else:
                    nc.scalar.activation(out=dst, in_=src, func=ACT.Copy, scale=t_sb[:, r : r + 1])

        def score(n, j):
            u, i, g = n // 4, (n // 2) % 2, n % 2
            r, m = (j, i) if u == 0 else (2 * i + j // 2, j % 2)
            pair, s = u % 2, u // 2
            rows = slice(g * ROWS, (g + 1) * ROWS)
            kcols = slice((1 - g) * ROWS, (1 - g) * ROWS + P)
            qcols = slice(m * Q, (m + 1) * Q)
            nc.tensor.matmul_mx(
                out=s_ps[g, i][:, j * Q : (j + 1) * Q],
                lhsT=k_codes[rows, r, kcols].bitcast(FP8X4),
                lhsT_scale=k_scales[rows, r, kcols],
                rhs=q_codes[pair, s][rows, qcols].bitcast(FP8X4),
                rhs_scale=q_scales[pair, s][rows, qcols],
                start=True,
                stop=True,
            )

        def scores(n):
            for j in range(2):
                work = [(n - 1, 2 + j), (n, j)]
                if n == 1:
                    work = [(j, 2 - 2 * j), (j, 3 - 2 * j)]
                for fill, part in work if n % 2 else reversed(work):
                    if 0 <= fill < 16:
                        score(fill, part)

        def sigmoids(n):
            u, i, g = n // 4, (n // 2) % 2, n % 2
            count = 4 if u == 0 else 2
            width = 4 * Q // count
            for j in range(count):
                r, a = (j, i * Q) if u == 0 else (2 * i + j, 0)
                nc.scalar.activation(
                    out=p_sb[2 * u + g][:, r, a : a + width],
                    in_=s_ps[g, i][:, j * width : (j + 1) * width],
                    func=ACT.Sigmoid,
                    bias=kb_sb[:, r : r + 1],
                )

        def weigh(b, a=0, z=2 * Q):
            s = blocks[b][1]
            nc.vector.tensor_tensor(
                out=w_bf[b][:, a:z, :].rearrange("p (c i) r -> p c r i", i=2),
                in0=p_sb[b][:, :, a:z].rearrange("p r (c i) -> p c r i", i=2),
                in1=tm[s][:, :, a:z].rearrange("p r (c i) -> p c r i", i=2),
                op=ALU.mult,
            )

        def quant_w(b, a=0, z=2 * Q):
            quant(w_codes[b][:, a:z], w_scales[b][:, a:z], w_bf[b][:, a:z, :].rearrange("p c r -> p (c r)"))

        def values(b, ms=range(2)):
            for m in ms:
                nc.tensor.matmul_mx(
                    out=y_ps[y_place[b][0]][:, y_place[b][1] + m, :],
                    lhsT=w_codes[b][:, m * Q : (m + 1) * Q].bitcast(FP8X4),
                    lhsT_scale=w_scales[b][:, m * Q : (m + 1) * Q],
                    rhs=v_codes[:].bitcast(FP8X4),
                    rhs_scale=v_scales[:],
                    start=True,
                    stop=True,
                )

        def sums(b):
            bank, slot = y_place[b]
            for m in range(2):
                nc.scalar.activation(out=squares[:, 2 * b + m, :], in_=y_ps[bank][:, slot + m, :], func=ACT.Square, accum_out=ssq[:, 2 * b + m : 2 * b + m + 1])

        def norms(a, z):
            nc.scalar.activation(out=rstd[:, 2 * a : 2 * z], in_=ssq[:, 2 * a : 2 * z], func=ACT.Abs_reciprocal_sqrt, scale=1.0 / E, bias=256.0 * EPS)

        def finish(b):
            bank, slot = y_place[b]
            for m in range(2):
                nc.vector.scalar_tensor_tensor(
                    out=o_sb[b][:, m, :], in0=y_ps[bank][:, slot + m, :], scalar=rstd[:, 2 * b + m : 2 * b + m + 1], in1=gn_sb[:], op0=ALU.mult, op1=ALU.mult
                )
            h, s = blocks[b]
            dst = out[h, s * 2 * Q : (s + 1) * 2 * Q, :].rearrange("(p m) e -> p m e", m=2)
            nc.sync.dma_start(out=dst, in_=o_sb[b][:])


        load_k()
        load_q(0, 0)
        nc.scalar.dma_start(out=kb_sb[:], in_=kb.rearrange("(p r) o -> p (r o)", r=PACK))
        nc.scalar.dma_start(out=t_sb[:], in_=t.rearrange("(p r) o -> p (r o)", r=PACK))
        load_q(1, 0)
        nc.vector.memset(warm_in[:], 0.0)
        nc.vector.memset(k_scales[:].bitcast(I32), 0)
        nc.scalar.activation(out=warm_out[:], in_=warm_in[:], func=ACT.Sigmoid)
        cast_k("v", 0, 40)
        cast_k("s", 40, 64)
        quant_k(0)
        quant_k(1)
        quant_k(2)
        quant_k(3)
        swap_k()
        load_mask(0)
        load_q(0, 1)
        load_q(1, 1)
        nc.sync.dma_start(out=v_raw[:], in_=v[0].rearrange("(p r) e -> p r e", r=PACK))
        load_mask(1)
        nc.sync.dma_start(out=gn_sb[:], in_=gn)
        cast_q("v", 0, 0)
        quant_q(0, 0)
        cast_q("v", 1, 0)
        quant_q(1, 0)
        make_tm("v", 0)
        scores(0)
        scores(1)
        scores(2)
        scores(3)
        sigmoids(0)
        scores(4)
        sigmoids(1)
        scores(5)
        sigmoids(2)
        scores(6)
        sigmoids(3)
        scores(7)
        weigh(0, 0, Q)
        cast_q("v", 0, 1)
        weigh(1, 0, Q)
        quant_q(0, 1)
        weigh(0, Q, 2 * Q)
        cast_q("v", 1, 1)
        weigh(1, Q, 2 * Q)
        quant_q(1, 1)
        interleave("v", v_bf[:], v_raw[:])
        quant_w(0)
        quant(v_codes[:], v_scales[:], v_bf[:].rearrange("p e r -> p (e r)"))
        sigmoids(4)
        scores(8)
        sigmoids(5)
        scores(9)
        sigmoids(6)
        scores(10)
        sigmoids(7)
        scores(11)
        sigmoids(8)
        scores(12)
        sigmoids(9)
        scores(13)
        weigh(2)
        quant_w(1)
        make_tm("v", 1, [0])
        make_tm("s", 1, [1, 2, 3])
        values(0)
        sigmoids(10)
        scores(14)
        values(1)
        sigmoids(11)
        scores(15)
        scores(16)
        weigh(3)
        quant_w(2)
        weigh(4)
        quant_w(3)
        values(2)
        values(3)
        sigmoids(12)
        sigmoids(13)
        sums(0)
        sigmoids(14)
        sums(1)
        sigmoids(15)
        sums(2)
        norms(0, 3)
        weigh(5)
        quant_w(4)
        values(4)
        weigh(6)
        quant_w(5)
        values(5)
        sums(3)
        weigh(7)
        quant_w(6)
        sums(4)
        sums(5)
        finish(0)
        values(6)
        quant_w(7)
        finish(1)
        values(7)
        norms(3, 5)
        sums(6)
        norms(5, 6)
        sums(7)
        norms(6, 7)
        norms(7, 8)
        finish(2)
        finish(3)
        finish(4)
        finish(5)
        finish(6)
        finish(7)
